import numpy as np
import ml_dtypes


def mxq(x, axis, fmt="e4m3"):
    dtype, down = {"e4m3": (ml_dtypes.float8_e4m3fn, 7), "e5m2": (ml_dtypes.float8_e5m2, 14)}[fmt]
    v = np.moveaxis(np.asarray(x, np.float32).astype(ml_dtypes.bfloat16).astype(np.float64), axis, -1)
    blocks = v.reshape(v.shape[:-1] + (-1, 32))
    amax = np.abs(blocks).max(-1, keepdims=True)
    byte = np.maximum(np.where(amax > 0, np.frexp(amax)[1] - 1 + 127, 0) - down, 1)
    scale = np.exp2(byte - 127.0)
    codes = (blocks / scale).astype(np.float32).astype(dtype).astype(np.float64)
    return np.moveaxis((codes * scale).reshape(v.shape), -1, axis)


WIDE = False


def mx_kscale(k):
    if not WIDE:
        return np.ones(k)
    levels = np.array([10, -10, 5, -5, 0])
    if k % 512:
        return np.exp2(np.random.permutation(np.resize(levels, k // 32))).repeat(32)
    a = np.empty((k // 512, 16))
    for p in range(k // 512):
        a[p, :8] = np.random.permutation(np.resize(levels, 8))
        for g in range(8):
            far = levels[np.abs(levels - a[p, g]) >= 10]
            a[p, g + 8] = far[np.random.randint(len(far))]
    return np.exp2(a.ravel()).repeat(32)


def f64(x):
    return np.asarray(x).astype(np.float64)


def striped(idx):
    return np.tile(idx.reshape(-1, 16).T, (8, 1)).astype(np.uint16)


def unstriped(offs):
    return offs[:16].T.reshape(-1).astype(np.int64)


def striped8(idx):
    return np.concatenate([x.reshape(-1, 16).T for x in idx]).astype(np.uint16)


def runs(offs, k):
    lists = np.stack([offs[16 * r : 16 * r + 16].T.reshape(-1) for r in range(8)]).astype(np.int64)
    return lists[np.arange(k) % 512 // 64]


def pack_weight(w):
    k, n = w.shape
    w = f64(np.asarray(w, np.float32).astype(ml_dtypes.bfloat16)).reshape(k // 32, 32, n)
    amax = np.abs(w).max(1)
    byte = np.clip(np.where(amax > 0, np.frexp(amax)[1] - 1 + 127 - 7, 1), 1, 254)
    scaled = (w * np.exp2(127.0 - byte)[:, None, :]).reshape(k, n).astype(np.float32)
    words = np.ascontiguousarray(scaled.reshape(k // 512, 128, 4, n).transpose(0, 1, 3, 2)).astype(ml_dtypes.float8_e4m3fn).view(np.uint8)
    return words, np.ascontiguousarray(byte.astype(np.uint8).reshape(k // 512, 16, n))


def unpack_weight(words, scales):
    g, p, n, _ = words.shape
    vals = np.ascontiguousarray(words).view(ml_dtypes.float8_e4m3fn).astype(np.float64) * np.repeat(np.exp2(scales.astype(np.float64) - 127.0), 8, axis=1)[..., None]
    return vals.transpose(0, 1, 3, 2).reshape(g * 512, n)


K, T, S, H, W, C, U = 512, 2048, 512, 512, 256, 512, 1024


def setup_inputs():
    n = np.random.standard_normal
    s = mx_kscale(K)[:, None]
    packed_xT = pack_weight(n((K, T)) * s)
    perm = np.stack([np.random.permutation(S) for _ in range(8)])
    return {
        "x_words": packed_xT[0],
        "x_scales": packed_xT[1],
        "w1": (n((K, H)) / np.sqrt(K) / s).astype(np.float32),
        "gs": (np.random.uniform(0.5, 1.5, (K, 1)) / s).astype(np.float32),
        "mem": n((C, U)).astype(np.float32),
        "offs": striped(np.random.permutation(T)[:S]),
        "n1": striped8(perm[:, :W]),
        "n2": striped8(perm[:, W:]),
        "n3": striped8(np.stack([np.random.permutation(S) for _ in range(8)])),
        "cand": striped(np.random.permutation(T)[:C]),
        "n4": striped8(np.stack([np.random.permutation(U)[:S] for _ in range(8)])),
        "n5": striped8(np.stack([np.random.permutation(U) for _ in range(8)])),
    }


def reference(x_words, x_scales, w1, gs, mem, offs, n1, n2, n3, cand, n4, n5):
    x_cand = unpack_weight(x_words, x_scales)[:, unstriped(cand)]
    xq = unpack_weight(x_words, x_scales)[:, unstriped(offs)]
    y = mxq(f64(w1), 0, "e4m3").T @ xq
    pa = y[np.arange(H)[:, None], runs(n1, H)]
    pb = y[np.arange(H)[:, None], runs(n2, H)]
    ra = pa - (0.5 * pb)
    ds = y.copy()
    ds[np.arange(H)[:, None], runs(n2, H)] = ra
    z = f64(gs) * (ds - (0.5 * (ds[np.arange(H)[:, None], runs(n3, H)])))
    s = 0.0625 * ((x_cand.T @ mxq(z, 0, "e4m3")))
    pg = f64(mem).copy()
    pg[np.arange(C)[:, None], runs(n4, C)] = s
    return pg - (0.5 * (pg[np.arange(C)[:, None], runs(n5, C)]))

@@ -1,0 +1,183 @@
+from contextlib import ExitStack
+
+import concourse.mybir as mybir
+
+K, T, S, H, W, C, U = 512, 2048, 512, 512, 256, 512, 1024
+FLOPS = 2 * K * H * S + 2 * K * C * S
+
+F32 = mybir.dt.float32
+BF16 = mybir.dt.bfloat16
+I32 = mybir.dt.int32
+U32 = mybir.dt.uint32
+U16 = mybir.dt.uint16
+U8 = mybir.dt.uint8
+FP8X4 = mybir.dt.float8_e4m3fn_x4
+MULT = mybir.AluOpType.mult
+ADD = mybir.AluOpType.add
+COPY = mybir.ActivationFunctionType.Copy
+
+P = 128
+PACK = 4
+RUN = 8
+HALF = S // 2
+PER_COL = 16
+
+
+def tile_picked_candfolddpagem_none_p_kernel(tc, x_words, x_scales, w1, gs, mem, offs, n1, n2, n3, cand, n4, n5, out):
+    nc = tc.nc
+    with ExitStack() as ctx:
+        keep = ctx.enter_context(tc.tile_pool(name="keep", bufs=1))
+        psum = ctx.enter_context(tc.psum_pool(name="psum", bufs=1))
+
+        def load_list(src, name):
+            tile = keep.tile(list(src.shape), U16, name=name)
+            nc.sync.dma_start(tile[:], src)
+            return tile
+
+        offs_sb = load_list(offs, "offs_sb")
+        cand_sb = load_list(cand, "cand_sb")
+
+        xs = keep.tile([P, T], U8, name="xs")
+        for q in range(4):
+            nc.scalar.dma_start(
+                xs[32 * q : 32 * (q + 1), :].bitcast(I32),
+                x_scales[0:1, 4 * q : 4 * (q + 1), :].bitcast(I32).to_broadcast([8, 4, T // 4]),
+            )
+
+        w_view = w1.rearrange("(p j) c -> p j c", j=PACK)
+        w_raw = []
+        for h in range(2):
+            raw = keep.tile([P, PACK, H // 2], F32, name="w_raw%d" % h)
+            nc.sync.dma_start(raw[:], w_view[:, :, h * (H // 2) : (h + 1) * (H // 2)])
+            w_raw.append(raw)
+
+        xw = keep.tile([P, T], I32, name="xw")
+        nc.sync.dma_start(xw[:], x_words[0].rearrange("p c r -> p (c r)").bitcast(I32))
+
+        gs_sb = keep.tile([P, PACK], F32, name="gs_sb")
+        nc.sync.dma_start(gs_sb[:], gs.rearrange("(p t) o -> p (t o)", t=PACK))
+        n1_sb = load_list(n1, "n1_sb")
+        n2_sb = load_list(n2, "n2_sb")
+        n3_sb = load_list(n3, "n3_sb")
+        n4_sb = load_list(n4, "n4_sb")
+        n5_sb = load_list(n5, "n5_sb")
+
+        mem_view = mem.rearrange("(a t b) w -> t a b w", t=PACK, b=RUN)
+        out_view = out.rearrange("(a t b) w -> t a b w", t=PACK, b=RUN)
+        page = []
+        for t in range(PACK):
+            pg = keep.tile([P, U], F32, name="page%d" % t)
+            nc.sync.dma_start(pg[:], mem_view[t])
+            page.append(pg)
+
+        xq_scales = keep.tile([P, S], U8, name="xq_scales", align_bytes=64)
+        nc.vector.tensor_copy(xq_scales[:], xs[:].indirect(offs_sb[:]))
+        xc_scales_listed = keep.tile([P, C], U8, name="xc_scales_listed", align_bytes=64)
+        nc.vector.tensor_copy(xc_scales_listed[:], xs[:].indirect(cand_sb[:]))
+        xc_scales = keep.tile([P, C], U8, name="xc_scales", align_bytes=64)
+        nc.vector.tensor_copy(
+            xc_scales[:].bitcast(I32).rearrange("p (t a b) -> p a t b", t=PACK, b=RUN // 4),
+            xc_scales_listed[:].bitcast(I32).rearrange("p (a t b) -> p a t b", t=PACK, b=RUN // 4),
+        )
+
+        w_grouped = keep.tile([P, H * PACK], BF16, name="w_grouped", align_bytes=64)
+        w_dealt = w_grouped[:].rearrange("p (t m j) -> p m t j", t=PACK, j=PACK)
+        for h in range(2):
+            nc.scalar.activation(
+                w_dealt[:, h * (P // 2) : (h + 1) * (P // 2)],
+                w_raw[h][:].rearrange("p j (m t) -> p m t j", t=PACK),
+                COPY,
+            )
+        w_codes = keep.tile([P, H], U32, name="w_codes", align_bytes=64)
+        w_scales = keep.tile([P, H], U8, name="w_scales", align_bytes=64)
+        nc.vector.quantize_mx(w_codes[:].bitcast(FP8X4), w_scales[:], w_grouped[:])
+
+        xq_words = keep.tile([P, S], U32, name="xq_words", align_bytes=64)
+        nc.vector.tensor_copy(xq_words[:], xw[:].bitcast(U32).indirect(offs_sb[:]))
+        xc_words = keep.tile([P, C], U32, name="xc_words", align_bytes=64)
+        nc.vector.tensor_copy(
+            xc_words[:].rearrange("p (t a b) -> p a t b", t=PACK, b=RUN),
+            xw[:].bitcast(U32).indirect(cand_sb[:]),
+        )
+
+        ds = []
+        for t in range(PACK):
+            cols = slice(t * P, (t + 1) * P)
+            y_ps = psum.tile([P, S], F32, name="y_ps%d" % t)
+            nc.tensor.matmul_mx(
+                y_ps[:], lhsT=w_codes[:, cols].bitcast(FP8X4), lhsT_scale=w_scales[:, cols],
+                rhs=xq_words[:].bitcast(FP8X4), rhs_scale=xq_scales[:], start=True, stop=True,
+            )
+            row = keep.tile([P, S], F32, name="ds%d" % t)
+            nc.scalar.activation(row[:], y_ps[:], COPY, scale=gs_sb[:, t : t + 1])
+            ds.append(row)
+
+        ds_half = []
+        for t in range(PACK):
+            pa = keep.tile([P, W], F32, name="pa%d" % t)
+            pb = keep.tile([P, W], F32, name="pb%d" % t)
+            nc.vector.tensor_copy(pa[:], ds[t][:].indirect(n1_sb[:]))
+            nc.vector.tensor_scalar(pb[:], ds[t][:].indirect(n2_sb[:]), -0.5, 0.0, MULT, ADD)
+            nc.vector.tensor_tensor(ds[t][:].indirect(n2_sb[:]), pa[:], pb[:], ADD)
+            scaled = keep.tile([P, S], F32, name="ds_half%d" % t)
+            nc.scalar.activation(scaled[:], ds[t][:], COPY, scale=-0.5)
+            ds_half.append(scaled)
+
+        s_ps = [psum.tile([P, S], F32, name="s_ps%d" % t) for t in range(PACK)]
+        score = [keep.tile([P, S], F32, name="score%d" % t) for t in range(PACK)]
+        for h in range(2):
+            cols = slice(h * HALF, (h + 1) * HALF)
+            lst = slice(h * HALF // PER_COL, (h + 1) * HALF // PER_COL)
+            z = keep.tile([P, PACK, HALF], F32, name="z%d" % h)
+            for t in range(PACK):
+                nc.vector.tensor_tensor(z[:, t, :], ds_half[t][:].indirect(n3_sb[:, lst]), ds[t][:, cols], ADD)
+            z_grouped = keep.tile([P, HALF * PACK], BF16, name="z_grouped%d" % h, align_bytes=64)
+            nc.scalar.activation(
+                z_grouped[:].rearrange("p (c i t) -> p c t i", i=4, t=PACK),
+                z[:].rearrange("p t (c i) -> p c t i", i=4),
+                COPY,
+            )
+            z_codes = keep.tile([P, HALF], U32, name="z_codes%d" % h, align_bytes=64)
+            z_scales = keep.tile([P, HALF], U8, name="z_scales%d" % h, align_bytes=64)
+            nc.vector.quantize_mx(z_codes[:].bitcast(FP8X4), z_scales[:], z_grouped[:])
+            for t in range(PACK):
+                rows = slice(t * P, (t + 1) * P)
+                nc.tensor.matmul_mx(
+                    s_ps[t][:, cols], lhsT=xc_words[:, rows].bitcast(FP8X4), lhsT_scale=xc_scales[:, rows],
+                    rhs=z_codes[:].bitcast(FP8X4), rhs_scale=z_scales[:], start=True, stop=True,
+                )
+                nc.scalar.activation(score[t][:, cols], s_ps[t][:, cols], COPY, scale=0.0625)
+
+        def write_scores(t, first, last):
+            nc.vector.tensor_copy(
+                page[t][:].indirect(n4_sb[:, first // PER_COL : last // PER_COL]), score[t][:, first:last]
+            )
+
+        page_half = {}
+
+        def scale_page(t):
+            page_half[t] = keep.tile([P, U], F32, name="page_half%d" % t)
+            nc.scalar.activation(page_half[t][:], page[t][:], COPY, scale=-0.5)
+
+        def read_page(t):
+            for h in range(2):
+                cols = slice(h * U // 2, (h + 1) * U // 2)
+                lst = slice(h * U // 2 // PER_COL, (h + 1) * U // 2 // PER_COL)
+                res = keep.tile([P, U // 2], F32, name="res%d_%d" % (t, h))
+                nc.vector.tensor_tensor(res[:], page_half[t][:].indirect(n5_sb[:, lst]), page[t][:, cols], ADD)
+                nc.sync.dma_start(out_view[t][:, :, cols], res[:])
+
+        write_scores(0, 0, HALF)
+        write_scores(1, 0, HALF)
+        write_scores(0, HALF, S)
+        scale_page(0)
+        write_scores(1, HALF, S)
+        scale_page(1)
+        read_page(0)
+        write_scores(2, 0, S)
+        scale_page(2)
+        read_page(1)
+        write_scores(3, 0, S)
+        scale_page(3)
+        read_page(2)
+        read_page(3)

@@ -12,8 +12,8 @@ U32 = mybir.dt.uint32
 U16 = mybir.dt.uint16
 U8 = mybir.dt.uint8
 FP8X4 = mybir.dt.float8_e4m3fn_x4
-MULT = mybir.AluOpType.mult
 ADD = mybir.AluOpType.add
+SUB = mybir.AluOpType.subtract
 COPY = mybir.ActivationFunctionType.Copy
 
 P = 128
@@ -34,22 +34,21 @@ def tile_picked_candfolddpagem_none_p_kernel(tc, x_words, x_scales, w1, gs, mem,
             nc.sync.dma_start(tile[:], src)
             return tile
 
-        offs_sb = load_list(offs, "offs_sb")
-        cand_sb = load_list(cand, "cand_sb")
-
-        xs = keep.tile([P, T], U8, name="xs")
-        for q in range(4):
-            nc.scalar.dma_start(
-                xs[32 * q : 32 * (q + 1), :].bitcast(I32),
-                x_scales[0:1, 4 * q : 4 * (q + 1), :].bitcast(I32).to_broadcast([8, 4, T // 4]),
-            )
-
         w_view = w1.rearrange("(p j) c -> p j c", j=PACK)
-        w_raw = []
-        for h in range(2):
+
+        def load_w(h):
             raw = keep.tile([P, PACK, H // 2], F32, name="w_raw%d" % h)
             nc.sync.dma_start(raw[:], w_view[:, :, h * (H // 2) : (h + 1) * (H // 2)])
-            w_raw.append(raw)
+            return raw
+
+        xs = keep.tile([P, T], U8, name="xs")
+        nc.vector.memset(xs[:].bitcast(I32), 0)
+        offs_sb = load_list(offs, "offs_sb")
+        w_raw = [load_w(0)]
+        for q in range(4):
+            nc.sync.dma_start(xs[32 * q : 32 * q + 4, :].bitcast(I32), x_scales[0, 4 * q : 4 * (q + 1), :].bitcast(I32))
+        cand_sb = load_list(cand, "cand_sb")
+        w_raw.append(load_w(1))
 
         xw = keep.tile([P, T], I32, name="xw")
         nc.sync.dma_start(xw[:], x_words[0].rearrange("p c r -> p (c r)").bitcast(I32))
@@ -93,7 +92,11 @@ def tile_picked_candfolddpagem_none_p_kernel(tc, x_words, x_scales, w1, gs, mem,
         nc.vector.quantize_mx(w_codes[:].bitcast(FP8X4), w_scales[:], w_grouped[:])
 
         xq_words = keep.tile([P, S], U32, name="xq_words", align_bytes=64)
-        nc.vector.tensor_copy(xq_words[:], xw[:].bitcast(U32).indirect(offs_sb[:]))
+        for h in range(2):
+            nc.vector.tensor_copy(
+                xq_words[:, h * HALF : (h + 1) * HALF],
+                xw[:].bitcast(U32).indirect(offs_sb[:, h * HALF // PER_COL : (h + 1) * HALF // PER_COL]),
+            )
         xc_words = keep.tile([P, C], U32, name="xc_words", align_bytes=64)
         nc.vector.tensor_copy(
             xc_words[:].rearrange("p (t a b) -> p a t b", t=PACK, b=RUN),
@@ -102,51 +105,78 @@ def tile_picked_candfolddpagem_none_p_kernel(tc, x_words, x_scales, w1, gs, mem,
 
         ds = []
         for t in range(PACK):
-            cols = slice(t * P, (t + 1) * P)
-            y_ps = psum.tile([P, S], F32, name="y_ps%d" % t)
-            nc.tensor.matmul_mx(
-                y_ps[:], lhsT=w_codes[:, cols].bitcast(FP8X4), lhsT_scale=w_scales[:, cols],
-                rhs=xq_words[:].bitcast(FP8X4), rhs_scale=xq_scales[:], start=True, stop=True,
-            )
+            rows = slice(t * P, (t + 1) * P)
             row = keep.tile([P, S], F32, name="ds%d" % t)
-            nc.scalar.activation(row[:], y_ps[:], COPY, scale=gs_sb[:, t : t + 1])
+            width = HALF if t == 0 else S
+            for first in range(0, S, width):
+                cols = slice(first, first + width)
+                y_ps = psum.tile([P, S], F32, name="y_ps", tag="bank%d" % (t + first // HALF + min(t, 1)))
+                nc.tensor.matmul_mx(
+                    y_ps[:, cols], lhsT=w_codes[:, rows].bitcast(FP8X4), lhsT_scale=w_scales[:, rows],
+                    rhs=xq_words[:, cols].bitcast(FP8X4), rhs_scale=xq_scales[:, cols], start=True, stop=True,
+                )
+                nc.scalar.activation(row[:, cols], y_ps[:, cols], COPY, scale=gs_sb[:, t : t + 1])
             ds.append(row)
 
-        ds_half = []
+        z = [keep.tile([P, PACK * HALF], F32, name="z0"), keep.tile([P, PACK * HALF], F32, name="z1", tag="late")]
         for t in range(PACK):
-            pa = keep.tile([P, W], F32, name="pa%d" % t)
+            if t < 2:
+                pa_tile = keep.tile([P, W], F32, name="pa%d" % t)
+                pa = pa_tile[:]
+            else:
+                pa = z[0][:, (t - 1) * HALF : t * HALF]
             pb = keep.tile([P, W], F32, name="pb%d" % t)
-            nc.vector.tensor_copy(pa[:], ds[t][:].indirect(n1_sb[:]))
-            nc.vector.tensor_scalar(pb[:], ds[t][:].indirect(n2_sb[:]), -0.5, 0.0, MULT, ADD)
-            nc.vector.tensor_tensor(ds[t][:].indirect(n2_sb[:]), pa[:], pb[:], ADD)
-            scaled = keep.tile([P, S], F32, name="ds_half%d" % t)
-            nc.scalar.activation(scaled[:], ds[t][:], COPY, scale=-0.5)
-            ds_half.append(scaled)
+            pb_half = keep.tile([P, W], F32, name="pb_half%d" % t)
+            nc.vector.tensor_copy(pb[:], ds[t][:].indirect(n2_sb[:]))
+            nc.vector.tensor_copy(pa, ds[t][:].indirect(n1_sb[:]))
+            nc.scalar.activation(pb_half[:], pb[:], COPY, scale=-0.5)
+            nc.vector.tensor_tensor(ds[t][:].indirect(n2_sb[:]), pa, pb_half[:], ADD)
 
-        s_ps = [psum.tile([P, S], F32, name="s_ps%d" % t) for t in range(PACK)]
-        score = [keep.tile([P, S], F32, name="score%d" % t) for t in range(PACK)]
-        for h in range(2):
+        s_ps = [psum.tile([P, S], F32, name="s_ps%d" % t, tag="bank%d" % ((5 + t) % 8)) for t in range(PACK)]
+        z_codes = keep.tile([P, S], U32, name="z_codes", align_bytes=64)
+        z_scales = keep.tile([P, S], U8, name="z_scales", align_bytes=64)
+
+        def make_z(h):
             cols = slice(h * HALF, (h + 1) * HALF)
             lst = slice(h * HALF // PER_COL, (h + 1) * HALF // PER_COL)
-            z = keep.tile([P, PACK, HALF], F32, name="z%d" % h)
             for t in range(PACK):
-                nc.vector.tensor_tensor(z[:, t, :], ds_half[t][:].indirect(n3_sb[:, lst]), ds[t][:, cols], ADD)
-            z_grouped = keep.tile([P, HALF * PACK], BF16, name="z_grouped%d" % h, align_bytes=64)
+                doubled = keep.tile([P, HALF], F32, name="doubled", bufs=3)
+                nc.scalar.activation(doubled[:], ds[t][:, cols], COPY, scale=2.0)
+                nc.vector.tensor_tensor(
+                    z[h][:, t * HALF : (t + 1) * HALF], ds[t][:].indirect(n3_sb[:, lst]), doubled[:], SUB
+                )
+            z_grouped = keep.tile([P, PACK * HALF], BF16, name="z_grouped%d" % h, align_bytes=64)
             nc.scalar.activation(
                 z_grouped[:].rearrange("p (c i t) -> p c t i", i=4, t=PACK),
-                z[:].rearrange("p t (c i) -> p c t i", i=4),
+                z[h][:].rearrange("p (t c i) -> p c t i", t=PACK, i=4),
                 COPY,
+                scale=-0.5,
             )
-            z_codes = keep.tile([P, HALF], U32, name="z_codes%d" % h, align_bytes=64)
-            z_scales = keep.tile([P, HALF], U8, name="z_scales%d" % h, align_bytes=64)
-            nc.vector.quantize_mx(z_codes[:].bitcast(FP8X4), z_scales[:], z_grouped[:])
-            for t in range(PACK):
-                rows = slice(t * P, (t + 1) * P)
-                nc.tensor.matmul_mx(
-                    s_ps[t][:, cols], lhsT=xc_words[:, rows].bitcast(FP8X4), lhsT_scale=xc_scales[:, rows],
-                    rhs=z_codes[:].bitcast(FP8X4), rhs_scale=z_scales[:], start=True, stop=True,
-                )
-                nc.scalar.activation(score[t][:, cols], s_ps[t][:, cols], COPY, scale=0.0625)
+            nc.vector.quantize_mx(z_codes[:, cols].bitcast(FP8X4), z_scales[:, cols], z_grouped[:])
+
+        score = {}
+
+        def make_scores(t, first, last):
+            rows = slice(t * P, (t + 1) * P)
+            cols = slice(first, last)
+            nc.tensor.matmul_mx(
+                s_ps[t][:, cols], lhsT=xc_words[:, rows].bitcast(FP8X4), lhsT_scale=xc_scales[:, rows],
+                rhs=z_codes[:, cols].bitcast(FP8X4), rhs_scale=z_scales[:, cols], start=True, stop=True,
+            )
+            nc.scalar.activation(score[t][:, cols], s_ps[t][:, cols], COPY, scale=0.0625)
+
+        make_z(0)
+        score[0] = keep.tile([P, S], F32, name="score0")
+        make_scores(0, 0, HALF)
+        make_z(1)
+        score[1] = keep.tile([P, S], F32, name="score1", tag="late")
+        score[2] = keep.tile([P, S], F32, name="score2")
+        score[3] = keep.tile([P, S], F32, name="score3")
+        make_scores(1, 0, HALF)
+        make_scores(0, HALF, S)
+        make_scores(1, HALF, S)
+        make_scores(2, 0, S)
+        make_scores(3, 0, S)
 
         def write_scores(t, first, last):
             nc.vector.tensor_copy(
@@ -160,11 +190,13 @@ def tile_picked_candfolddpagem_none_p_kernel(tc, x_words, x_scales, w1, gs, mem,
             nc.scalar.activation(page_half[t][:], page[t][:], COPY, scale=-0.5)
 
         def read_page(t):
-            for h in range(2):
-                cols = slice(h * U // 2, (h + 1) * U // 2)
-                lst = slice(h * U // 2 // PER_COL, (h + 1) * U // 2 // PER_COL)
-                res = keep.tile([P, U // 2], F32, name="res%d_%d" % (t, h))
-                nc.vector.tensor_tensor(res[:], page_half[t][:].indirect(n5_sb[:, lst]), page[t][:, cols], ADD)
+            edges = (0, U // 2, U) if t < PACK - 1 else (0, U // 2, 3 * U // 4, U)
+            for first, last in zip(edges, edges[1:]):
+                cols = slice(first, last)
+                res = keep.tile([P, last - first], F32, name="res%d_%d" % (t, first))
+                nc.vector.tensor_tensor(
+                    res[:], page_half[t][:].indirect(n5_sb[:, first // PER_COL : last // PER_COL]), page[t][:, cols], ADD
+                )
                 nc.sync.dma_start(out_view[t][:, :, cols], res[:])
 
         write_scores(0, 0, HALF)

@@ -136,22 +136,30 @@ def tile_picked_candfolddpagem_none_p_kernel(tc, x_words, x_scales, w1, gs, mem,
         z_codes = keep.tile([P, S], U32, name="z_codes", align_bytes=64)
         z_scales = keep.tile([P, S], U8, name="z_scales", align_bytes=64)
 
-        def make_z(h):
+        def make_z(h, pieces):
             cols = slice(h * HALF, (h + 1) * HALF)
-            lst = slice(h * HALF // PER_COL, (h + 1) * HALF // PER_COL)
+            z_grouped = keep.tile([P, PACK * HALF], BF16, name="z_grouped%d" % h, align_bytes=64)
+            planes = z[h][:].rearrange("p (t n) -> p t n", t=PACK)
             for t in range(PACK):
                 doubled = keep.tile([P, HALF], F32, name="doubled", bufs=3)
                 nc.scalar.activation(doubled[:], ds[t][:, cols], COPY, scale=2.0)
-                nc.vector.tensor_tensor(
-                    z[h][:, t * HALF : (t + 1) * HALF], ds[t][:].indirect(n3_sb[:, lst]), doubled[:], SUB
-                )
-            z_grouped = keep.tile([P, PACK * HALF], BF16, name="z_grouped%d" % h, align_bytes=64)
-            nc.scalar.activation(
-                z_grouped[:].rearrange("p (c i t) -> p c t i", i=4, t=PACK),
-                z[h][:].rearrange("p (t c i) -> p c t i", t=PACK, i=4),
-                COPY,
-                scale=-0.5,
-            )
+                width = HALF // pieces if t == PACK - 1 else HALF
+                for first in range(0, HALF, width):
+                    part = slice(first, first + width)
+                    entry = h * HALF + first
+                    nc.vector.tensor_tensor(
+                        planes[:, t, part],
+                        ds[t][:].indirect(n3_sb[:, entry // PER_COL : (entry + width) // PER_COL]),
+                        doubled[:, part],
+                        SUB,
+                    )
+                    if t == PACK - 1:
+                        nc.scalar.activation(
+                            z_grouped[:, first * PACK : (first + width) * PACK].rearrange("p (c i t) -> p c t i", i=4, t=PACK),
+                            planes[:, :, part].rearrange("p t (c i) -> p c t i", i=4),
+                            COPY,
+                            scale=-0.5,
+                        )
             nc.vector.quantize_mx(z_codes[:, cols].bitcast(FP8X4), z_scales[:, cols], z_grouped[:])
 
         score = {}
@@ -165,10 +173,10 @@ def tile_picked_candfolddpagem_none_p_kernel(tc, x_words, x_scales, w1, gs, mem,
             )
             nc.scalar.activation(score[t][:, cols], s_ps[t][:, cols], COPY, scale=0.0625)
 
-        make_z(0)
+        make_z(0, 2)
         score[0] = keep.tile([P, S], F32, name="score0")
         make_scores(0, 0, HALF)
-        make_z(1)
+        make_z(1, 1)
         score[1] = keep.tile([P, S], F32, name="score1", tag="late")
         score[2] = keep.tile([P, S], F32, name="score2")
         score[3] = keep.tile([P, S], F32, name="score3")

@@ -45,7 +45,7 @@ def tile_picked_candfolddpagem_none_p_kernel(tc, x_words, x_scales, w1, gs, mem,
         nc.vector.memset(xs[:].bitcast(I32), 0)
         offs_sb = load_list(offs, "offs_sb")
         w_raw = [load_w(0)]
-        for q in range(4):
+        for q in (0, 2, 1, 3):
             nc.sync.dma_start(xs[32 * q : 32 * q + 4, :].bitcast(I32), x_scales[0, 4 * q : 4 * (q + 1), :].bitcast(I32))
         cand_sb = load_list(cand, "cand_sb")
         w_raw.append(load_w(1))
@@ -176,7 +176,7 @@ def tile_picked_candfolddpagem_none_p_kernel(tc, x_words, x_scales, w1, gs, mem,
         make_z(0, 2)
         score[0] = keep.tile([P, S], F32, name="score0")
         make_scores(0, 0, HALF)
-        make_z(1, 1)
+        make_z(1, 2)
         score[1] = keep.tile([P, S], F32, name="score1", tag="late")
         score[2] = keep.tile([P, S], F32, name="score2")
         score[3] = keep.tile([P, S], F32, name="score3")

from contextlib import ExitStack

import concourse.mybir as mybir

K, T, S, H, W, C, U = 512, 2048, 512, 512, 256, 512, 1024
FLOPS = 2 * K * H * S + 2 * K * C * S

F32 = mybir.dt.float32
BF16 = mybir.dt.bfloat16
I32 = mybir.dt.int32
U32 = mybir.dt.uint32
U16 = mybir.dt.uint16
U8 = mybir.dt.uint8
FP8X4 = mybir.dt.float8_e4m3fn_x4
ADD = mybir.AluOpType.add
SUB = mybir.AluOpType.subtract
COPY = mybir.ActivationFunctionType.Copy

P = 128
PACK = 4
RUN = 8
HALF = S // 2
PER_COL = 16


def tile_picked_candfolddpagem_none_p_kernel(tc, x_words, x_scales, w1, gs, mem, offs, n1, n2, n3, cand, n4, n5, out):
    nc = tc.nc
    with ExitStack() as ctx:
        keep = ctx.enter_context(tc.tile_pool(name="keep", bufs=1))
        psum = ctx.enter_context(tc.psum_pool(name="psum", bufs=1))

        def load_list(src, name):
            tile = keep.tile(list(src.shape), U16, name=name)
            nc.sync.dma_start(tile[:], src)
            return tile

        w_view = w1.rearrange("(p j) c -> p j c", j=PACK)

        def load_w(h):
            raw = keep.tile([P, PACK, H // 2], F32, name="w_raw%d" % h)
            nc.sync.dma_start(raw[:], w_view[:, :, h * (H // 2) : (h + 1) * (H // 2)])
            return raw

        xs = keep.tile([P, T], U8, name="xs")
        nc.vector.memset(xs[:].bitcast(I32), 0)
        offs_sb = load_list(offs, "offs_sb")
        w_raw = [load_w(0)]
        for q in (0, 2, 1, 3):
            nc.sync.dma_start(xs[32 * q : 32 * q + 4, :].bitcast(I32), x_scales[0, 4 * q : 4 * (q + 1), :].bitcast(I32))
        cand_sb = load_list(cand, "cand_sb")
        w_raw.append(load_w(1))

        xw = keep.tile([P, T], I32, name="xw")
        nc.sync.dma_start(xw[:], x_words[0].rearrange("p c r -> p (c r)").bitcast(I32))

        gs_sb = keep.tile([P, PACK], F32, name="gs_sb")
        nc.sync.dma_start(gs_sb[:], gs.rearrange("(p t) o -> p (t o)", t=PACK))
        n1_sb = load_list(n1, "n1_sb")
        n2_sb = load_list(n2, "n2_sb")
        n3_sb = load_list(n3, "n3_sb")
        n4_sb = load_list(n4, "n4_sb")
        n5_sb = load_list(n5, "n5_sb")

        mem_view = mem.rearrange("(a t b) w -> t a b w", t=PACK, b=RUN)
        out_view = out.rearrange("(a t b) w -> t a b w", t=PACK, b=RUN)
        page = []
        for t in range(PACK):
            pg = keep.tile([P, U], F32, name="page%d" % t)
            nc.sync.dma_start(pg[:], mem_view[t])
            page.append(pg)

        xq_scales = keep.tile([P, S], U8, name="xq_scales", align_bytes=64)
        nc.vector.tensor_copy(xq_scales[:], xs[:].indirect(offs_sb[:]))
        xc_scales_listed = keep.tile([P, C], U8, name="xc_scales_listed", align_bytes=64)
        nc.vector.tensor_copy(xc_scales_listed[:], xs[:].indirect(cand_sb[:]))
        xc_scales = keep.tile([P, C], U8, name="xc_scales", align_bytes=64)
        nc.vector.tensor_copy(
            xc_scales[:].bitcast(I32).rearrange("p (t a b) -> p a t b", t=PACK, b=RUN // 4),
            xc_scales_listed[:].bitcast(I32).rearrange("p (a t b) -> p a t b", t=PACK, b=RUN // 4),
        )

        w_grouped = keep.tile([P, H * PACK], BF16, name="w_grouped", align_bytes=64)
        w_dealt = w_grouped[:].rearrange("p (t m j) -> p m t j", t=PACK, j=PACK)
        for h in range(2):
            nc.scalar.activation(
                w_dealt[:, h * (P // 2) : (h + 1) * (P // 2)],
                w_raw[h][:].rearrange("p j (m t) -> p m t j", t=PACK),
                COPY,
            )
        w_codes = keep.tile([P, H], U32, name="w_codes", align_bytes=64)
        w_scales = keep.tile([P, H], U8, name="w_scales", align_bytes=64)
        nc.vector.quantize_mx(w_codes[:].bitcast(FP8X4), w_scales[:], w_grouped[:])

        xq_words = keep.tile([P, S], U32, name="xq_words", align_bytes=64)
        for h in range(2):
            nc.vector.tensor_copy(
                xq_words[:, h * HALF : (h + 1) * HALF],
                xw[:].bitcast(U32).indirect(offs_sb[:, h * HALF // PER_COL : (h + 1) * HALF // PER_COL]),
            )
        xc_words = keep.tile([P, C], U32, name="xc_words", align_bytes=64)
        nc.vector.tensor_copy(
            xc_words[:].rearrange("p (t a b) -> p a t b", t=PACK, b=RUN),
            xw[:].bitcast(U32).indirect(cand_sb[:]),
        )

        ds = []
        for t in range(PACK):
            rows = slice(t * P, (t + 1) * P)
            row = keep.tile([P, S], F32, name="ds%d" % t)
            width = HALF if t == 0 else S
            for first in range(0, S, width):
                cols = slice(first, first + width)
                y_ps = psum.tile([P, S], F32, name="y_ps", tag="bank%d" % (t + first // HALF + min(t, 1)))
                nc.tensor.matmul_mx(
                    y_ps[:, cols], lhsT=w_codes[:, rows].bitcast(FP8X4), lhsT_scale=w_scales[:, rows],
                    rhs=xq_words[:, cols].bitcast(FP8X4), rhs_scale=xq_scales[:, cols], start=True, stop=True,
                )
                nc.scalar.activation(row[:, cols], y_ps[:, cols], COPY, scale=gs_sb[:, t : t + 1])
            ds.append(row)

        z = [keep.tile([P, PACK * HALF], F32, name="z0"), keep.tile([P, PACK * HALF], F32, name="z1", tag="late")]
        for t in range(PACK):
            if t < 2:
                pa_tile = keep.tile([P, W], F32, name="pa%d" % t)
                pa = pa_tile[:]
            else:
                pa = z[0][:, (t - 1) * HALF : t * HALF]
            pb = keep.tile([P, W], F32, name="pb%d" % t)
            pb_half = keep.tile([P, W], F32, name="pb_half%d" % t)
            nc.vector.tensor_copy(pb[:], ds[t][:].indirect(n2_sb[:]))
            nc.vector.tensor_copy(pa, ds[t][:].indirect(n1_sb[:]))
            nc.scalar.activation(pb_half[:], pb[:], COPY, scale=-0.5)
            nc.vector.tensor_tensor(ds[t][:].indirect(n2_sb[:]), pa, pb_half[:], ADD)

        s_ps = [psum.tile([P, S], F32, name="s_ps%d" % t, tag="bank%d" % ((5 + t) % 8)) for t in range(PACK)]
        z_codes = keep.tile([P, S], U32, name="z_codes", align_bytes=64)
        z_scales = keep.tile([P, S], U8, name="z_scales", align_bytes=64)

        def make_z(h, pieces):
            cols = slice(h * HALF, (h + 1) * HALF)
            z_grouped = keep.tile([P, PACK * HALF], BF16, name="z_grouped%d" % h, align_bytes=64)
            planes = z[h][:].rearrange("p (t n) -> p t n", t=PACK)
            for t in range(PACK):
                doubled = keep.tile([P, HALF], F32, name="doubled", bufs=3)
                nc.scalar.activation(doubled[:], ds[t][:, cols], COPY, scale=2.0)
                width = HALF // pieces if t == PACK - 1 else HALF
                for first in range(0, HALF, width):
                    part = slice(first, first + width)
                    entry = h * HALF + first
                    nc.vector.tensor_tensor(
                        planes[:, t, part],
                        ds[t][:].indirect(n3_sb[:, entry // PER_COL : (entry + width) // PER_COL]),
                        doubled[:, part],
                        SUB,
                    )
                    if t == PACK - 1:
                        nc.scalar.activation(
                            z_grouped[:, first * PACK : (first + width) * PACK].rearrange("p (c i t) -> p c t i", i=4, t=PACK),
                            planes[:, :, part].rearrange("p t (c i) -> p c t i", i=4),
                            COPY,
                            scale=-0.5,
                        )
            nc.vector.quantize_mx(z_codes[:, cols].bitcast(FP8X4), z_scales[:, cols], z_grouped[:])

        score = {}

        def make_scores(t, first, last):
            rows = slice(t * P, (t + 1) * P)
            cols = slice(first, last)
            nc.tensor.matmul_mx(
                s_ps[t][:, cols], lhsT=xc_words[:, rows].bitcast(FP8X4), lhsT_scale=xc_scales[:, rows],
                rhs=z_codes[:, cols].bitcast(FP8X4), rhs_scale=z_scales[:, cols], start=True, stop=True,
            )
            nc.scalar.activation(score[t][:, cols], s_ps[t][:, cols], COPY, scale=0.0625)

        make_z(0, 2)
        score[0] = keep.tile([P, S], F32, name="score0")
        make_scores(0, 0, HALF)
        make_z(1, 2)
        score[1] = keep.tile([P, S], F32, name="score1", tag="late")
        score[2] = keep.tile([P, S], F32, name="score2")
        score[3] = keep.tile([P, S], F32, name="score3")
        make_scores(1, 0, HALF)
        make_scores(0, HALF, S)
        make_scores(1, HALF, S)
        make_scores(2, 0, S)
        make_scores(3, 0, S)

        def write_scores(t, first, last):
            nc.vector.tensor_copy(
                page[t][:].indirect(n4_sb[:, first // PER_COL : last // PER_COL]), score[t][:, first:last]
            )

        page_half = {}

        def scale_page(t):
            page_half[t] = keep.tile([P, U], F32, name="page_half%d" % t)
            nc.scalar.activation(page_half[t][:], page[t][:], COPY, scale=-0.5)

        def read_page(t):
            edges = (0, U // 2, U) if t < PACK - 1 else (0, U // 2, 3 * U // 4, U)
            for first, last in zip(edges, edges[1:]):
                cols = slice(first, last)
                res = keep.tile([P, last - first], F32, name="res%d_%d" % (t, first))
                nc.vector.tensor_tensor(
                    res[:], page_half[t][:].indirect(n5_sb[:, first // PER_COL : last // PER_COL]), page[t][:, cols], ADD
                )
                nc.sync.dma_start(out_view[t][:, :, cols], res[:])

        write_scores(0, 0, HALF)
        write_scores(1, 0, HALF)
        write_scores(0, HALF, S)
        scale_page(0)
        write_scores(1, HALF, S)
        scale_page(1)
        read_page(0)
        write_scores(2, 0, S)
        scale_page(2)
        read_page(1)
        write_scores(3, 0, S)
        scale_page(3)
        read_page(2)
        read_page(3)
